import numpy as np, ml_dtypes
CORES = [8,11,14,16,19,22,24,27,30]
N = 9
DEG, TK, TIMES = 3, 128, 2
MASK = [[8,0,1],[0,1,2],[1,2,3],[2,3,4],[3,4,5],[4,5,6],[5,6,7],[6,7,8],[7,8,0]]
def setup_inputs(rng):
    return {"x": rng.standard_normal((N, 128, TK), dtype=np.float32).astype(ml_dtypes.bfloat16), "w": (rng.standard_normal((N, 128, DEG * 128), dtype=np.float32) / np.float32(np.sqrt(128 * DEG / 2))).astype(ml_dtypes.bfloat16)}
def setup_inputs_big(rng):
    d = setup_inputs(rng)
    for k in ("x", "w"): d[k] = (d[k].astype(np.float32) * 1024.0).astype(d[k].dtype)
    return d
def setup_inputs_small(rng):
    d = setup_inputs(rng)
    for k in ("x", "w"): d[k] = (d[k].astype(np.float32) * (1 / 1024.0)).astype(d[k].dtype)
    return d
def setup_inputs_apart(rng):
    d = setup_inputs(rng)
    f = (10.0 ** rng.permutation(np.linspace(-1.5, 1.5, N))).astype(np.float32).reshape(N, 1, 1)
    for k in ("x", "w"): d[k] = (d[k].astype(np.float32) * f).astype(d[k].dtype)
    return d
def reference(x, w):
    X, W = x.astype(np.float64), w.astype(np.float64)
    h = list(X)
    for _ in range(TIMES):
        h = [sum(W[r][:, 128 * i:128 * i + 128].T @ h[j] for i, j in enumerate(MASK[r])) for r in range(N)]
    return {"y": np.stack(h).astype(ml_dtypes.bfloat16)}

@@ -1,0 +1,193 @@
+from concourse.bass import DstId, RemoteDMATransfer
+
+K = 128
+
+SCRATCH = {
+    "wsb": ("sbuf", [K, 3 * K], "bfloat16"),
+    "xin": ("sbuf", [K, 3 * K], "bfloat16"),
+    "hin": ("sbuf", [K, 3 * K], "bfloat16"),
+    "hp": ("sbuf", [K, 2 * K], "bfloat16"),
+    "aw": ("sbuf", [K, K], "bfloat16"),
+    "ax": ("sbuf", [K, K], "bfloat16"),
+    "wb": ("sbuf", [K, 3 * K], "bfloat16"),
+    "zw": ("sbuf", [K, K], "bfloat16"),
+    "bx": ("sbuf", [K, K], "bfloat16"),
+    "zp": ("sbuf", [K, K], "bfloat16"),
+    "yo": ("sbuf", [K, K], "bfloat16"),
+    "ph": ("psum", [K, 512], "float32"),
+    "pb": ("psum", [K, 512], "float32"),
+    "pp": ("psum", [K, 512], "float32"),
+    "py": ("psum", [K, 512], "float32"),
+}
+SEMAPHORES = ["ldx", "ldw", "st", "sent", "sx0", "sx1", "sx2", "sh0", "sh1", "sh2",
+              "s_aw", "s_ax", "s_wb", "s_zw", "s_bx", "s_hp",
+              "m_h", "m_b", "m_p", "m_y", "v_h", "v_b", "v_p", "v_y"]
+
+
+def rank_program(g, core, T, topo):
+    r = T.rank_of(core)
+    if r is None:
+        return
+    M = T.tables["MASK"]
+    cores = T.cores
+    n = len(cores)
+
+    def ok(s, d):
+        return topo.may_write(cores[s], cores[d])
+
+    def ti(q, j):
+        return M[q].index(j)
+
+    def col(i):
+        return slice(i * K, (i + 1) * K)
+
+    users = [[q for q in range(n) if j in M[q] and q != j] for j in range(n)]
+
+    as_a, as_b, as_c, as_z = {}, {}, {}, {}
+    for a in range(n):
+        for b in M[a]:
+            if b != a and not ok(b, a):
+                zs = [q for q in users[a] if q != b]
+                assert len(zs) == 1
+                cs = [c for c in users[b] if c != a and ok(b, c) and ok(c, a) and ok(c, b) and ok(a, c)
+                      and ok(c, zs[0]) and topo.chip(cores[c]) == topo.chip(cores[b])]
+                bd = (zs[0], a, b, cs[0])
+                as_z[bd[0]], as_a[a], as_b[b], as_c[bd[3]] = bd, bd, bd, bd
+
+    lo_m, all_m = None, 0
+    for d in cores:
+        if d != core:
+            m = topo.mask(core, d)
+            lo_m = m if lo_m is None else (lo_m & m)
+            all_m |= m
+    hi_m = all_m & ~lo_m
+    E = bin(lo_m).count("1")
+    assert bin(hi_m).count("1") == E
+
+    sent = [0]
+    waited = {}
+
+    def need(qname, queue, sem, val):
+        if waited.get((qname, sem), 0) < val:
+            queue.wait_ge(T.sem[sem], val)
+            waited[(qname, sem)] = val
+
+    def send(items):
+        far = [it for it in items if topo.chip(cores[it[1]]) != topo.chip(core)]
+        near = [it for it in items if topo.chip(cores[it[1]]) == topo.chip(core)]
+        assert len(far) <= 1 and 1 <= len(items) <= 2
+        if far:
+            pairs = [(far[0], lo_m)] + [(it, hi_m) for it in near]
+        elif len(near) == 2:
+            pairs = [(near[0], lo_m), (near[1], hi_m)]
+        else:
+            pairs = [(near[0], hi_m)]
+        trs = []
+        for (src, q, dst, sem), m in pairs:
+            rid, pid, _se = topo.addr(cores[q])
+            trs.append(RemoteDMATransfer(dst_ids=[DstId(rid=rid, pnc=pid)], dma_engine_mask=m,
+                                         remote_sem=T.sem[sem], src=src, dst=dst))
+            sent[0] += E
+        g.remote_dma_fused(trs, local_sem=T.sem.sent)
+
+    own = ti(r, r)
+    te, ve = g.tensor, g.vector
+
+    g.sync.dma_start(T.xin[:, col(own)], T.x[:]).then_inc(T.sem.ldx, 16)
+    g.scalar.dma_start(T.wsb[:], T.w[:]).then_inc(T.sem.ldw, 16)
+
+    need("g", g, "ldx", 16)
+    items = [(T.xin[:, col(own)], q, T.xin[:, col(ti(q, r))], "sx%d" % ti(q, r))
+             for q in users[r] if ok(r, q) and q not in as_b]
+    if r in as_a:
+        items.append((T.xin[:, col(own)], as_a[r][3], T.ax[:], "s_ax"))
+    send(items)
+    if r in as_a:
+        z, a, b, c = as_a[r]
+        need("g", g, "ldw", 16)
+        send([(T.wsb[:, col(ti(a, b))], z, T.zw[:], "s_zw"), (T.wsb[:, col(ti(a, b))], c, T.aw[:], "s_aw")])
+    if r in as_b:
+        need("g", g, "ldw", 16)
+        send([(T.wsb[:], as_b[r][3], T.wb[:], "s_wb")])
+    if r in as_c:
+        z, a, b, c = as_c[r]
+        need("g", g, "sx%d" % ti(c, b), E)
+        send([(T.xin[:, col(ti(c, b))], z, T.bx[:], "s_bx")])
+    if r not in as_b:
+        need("g", g, "v_h", 1)
+        send([(T.hin[:, col(own)], q, T.hin[:, col(ti(q, r))], "sh%d" % ti(q, r)) for q in users[r]])
+    if r in as_c:
+        z, a, b, c = as_c[r]
+        need("g", g, "v_b", 1)
+        send([(T.hp[:], a, T.hp[:], "s_hp"), (T.hp[:], b, T.hp[:], "s_hp")])
+    g.wait_ge(T.sem.sent, sent[0])
+
+    def group(out, terms, done):
+        terms = sorted(terms, key=lambda t: t[0])
+        for k, (_o, lhsT, rhs, ws) in enumerate(terms):
+            for s, v in ws:
+                need("t", te, s, v)
+            ins = te.matmul(out, lhsT, rhs, k == 0, k == len(terms) - 1)
+            if done is not None and k == len(terms) - 1:
+                ins.then_inc(T.sem[done], 1)
+
+    def far_from(j):
+        return topo.chip(cores[j]) != topo.chip(core)
+
+    need("t", te, "ldw", 16)
+    if r not in as_b:
+        terms = []
+        for i, j in enumerate(M[r]):
+            if j == r:
+                terms.append((0, T.wsb[:, col(i)], T.xin[:, col(i)], [("ldx", 16)]))
+            elif ok(j, r):
+                terms.append((2 if far_from(j) else 1, T.wsb[:, col(i)], T.xin[:, col(i)], [("sx%d" % i, E)]))
+        group(T.ph[:, 0:K], terms, "m_h")
+        ve.wait_ge(T.sem.m_h, 1)
+        ve.tensor_copy(T.hin[:, col(own)], T.ph[:, 0:K]).then_inc(T.sem.v_h, 1)
+    if r in as_c:
+        z, a, b, c = as_c[r]
+        xb = T.xin[:, col(ti(c, b))]
+        xb_w = ("sx%d" % ti(c, b), E)
+        terms = []
+        for i, j in enumerate(M[b]):
+            if j == b:
+                terms.append((0, T.wb[:, col(i)], xb, [("s_wb", E), xb_w]))
+            elif j == c:
+                terms.append((1, T.wb[:, col(i)], T.xin[:, col(own)], [("s_wb", E), ("ldx", 16)]))
+            else:
+                assert j == a
+                terms.append((2, T.wb[:, col(i)], T.ax[:], [("s_wb", E), ("s_ax", E)]))
+        group(T.pb[:, 0:K], terms, None)
+        group(T.pb[:, K:2 * K], [(0, T.aw[:], xb, [("s_aw", E), xb_w])], "m_b")
+        ve.wait_ge(T.sem.m_b, 1)
+        ve.tensor_copy(T.hp[:], T.pb[:, 0:2 * K]).then_inc(T.sem.v_b, 1)
+    if r in as_z:
+        group(T.pp[:, 0:K], [(0, T.zw[:], T.bx[:], [("s_zw", E), ("s_bx", E)])], "m_p")
+        ve.wait_ge(T.sem.m_p, 1)
+        ve.tensor_copy(T.zp[:], T.pp[:, 0:K]).then_inc(T.sem.v_p, 1)
+
+    terms = []
+    for i, j in enumerate(M[r]):
+        w_i = T.wsb[:, col(i)]
+        if j in as_b:
+            if r == as_b[j][3]:
+                terms.append((1, w_i, T.hp[:, 0:K], [("v_b", 1)]))
+            else:
+                terms.append((5, w_i, T.hp[:, 0:K], [("s_hp", E)]))
+        elif j == r:
+            terms.append((0, w_i, T.hin[:, col(i)], [("v_h", 1)]))
+        else:
+            terms.append((3 if far_from(j) else 2, w_i, T.hin[:, col(i)], [("sh%d" % i, E)]))
+        if j in as_a:
+            if r == as_a[j][0]:
+                terms.append((4, w_i, T.zp[:], [("v_p", 1)]))
+            else:
+                terms.append((5, w_i, T.hp[:, K:2 * K], [("s_hp", E)]))
+    group(T.py[:, 0:K], terms, "m_y")
+    ve.wait_ge(T.sem.m_y, 1)
+    ve.tensor_copy(T.yo[:], T.py[:, 0:K]).then_inc(T.sem.v_y, 1)
+
+    g.sync.wait_ge(T.sem.v_y, 1)
+    g.sync.dma_start(T.y[:], T.yo[:]).then_inc(T.sem.st, 16)
+    g.sync.wait_ge(T.sem.st, 16)

@@ -1,17 +1,18 @@
 from concourse.bass import DstId, RemoteDMATransfer
 
 K = 128
+N = 9
 
 SCRATCH = {
     "wsb": ("sbuf", [K, 3 * K], "bfloat16"),
     "xin": ("sbuf", [K, 3 * K], "bfloat16"),
     "hin": ("sbuf", [K, 3 * K], "bfloat16"),
-    "hp": ("sbuf", [K, 2 * K], "bfloat16"),
-    "aw": ("sbuf", [K, K], "bfloat16"),
+    "hb": ("sbuf", [K, K], "bfloat16"),
     "ax": ("sbuf", [K, K], "bfloat16"),
     "wb": ("sbuf", [K, 3 * K], "bfloat16"),
     "zw": ("sbuf", [K, K], "bfloat16"),
     "bx": ("sbuf", [K, K], "bfloat16"),
+    "dx": ("sbuf", [K, K], "bfloat16"),
     "zp": ("sbuf", [K, K], "bfloat16"),
     "yo": ("sbuf", [K, K], "bfloat16"),
     "ph": ("psum", [K, 512], "float32"),
@@ -19,9 +20,8 @@ SCRATCH = {
     "pp": ("psum", [K, 512], "float32"),
     "py": ("psum", [K, 512], "float32"),
 }
-SEMAPHORES = ["ldx", "ldw", "st", "sent", "sx0", "sx1", "sx2", "sh0", "sh1", "sh2",
-              "s_aw", "s_ax", "s_wb", "s_zw", "s_bx", "s_hp",
-              "m_h", "m_b", "m_p", "m_y", "v_h", "v_b", "v_p", "v_y"]
+SEMAPHORES = (["ldx", "ldw", "st", "sent", "m_h", "m_b", "m_p", "m_y", "v_h", "v_b", "v_p", "v_y"]
+              + ["%s%d" % (k, j) for k in "XWFHP" for j in range(N)])
 
 
 def rank_program(g, core, T, topo):
@@ -41,23 +41,28 @@ def rank_program(g, core, T, topo):
     def col(i):
         return slice(i * K, (i + 1) * K)
 
+    def far_from(j):
+        return topo.chip(cores[j]) != topo.chip(core)
+
     users = [[q for q in range(n) if j in M[q] and q != j] for j in range(n)]
 
-    as_a, as_b, as_c, as_z = {}, {}, {}, {}
+    as_a, as_b, as_c, as_z, as_d = {}, {}, {}, {}, {}
     for a in range(n):
         for b in M[a]:
             if b != a and not ok(b, a):
                 zs = [q for q in users[a] if q != b]
                 assert len(zs) == 1
-                cs = [c for c in users[b] if c != a and ok(b, c) and ok(c, a) and ok(c, b) and ok(a, c)
-                      and ok(c, zs[0]) and topo.chip(cores[c]) == topo.chip(cores[b])]
-                bd = (zs[0], a, b, cs[0])
-                as_z[bd[0]], as_a[a], as_b[b], as_c[bd[3]] = bd, bd, bd, bd
+                home = [q for q in range(n) if q != b and topo.chip(cores[q]) == topo.chip(cores[b]) and ok(q, a)]
+                cs = [c for c in home if c in users[b] and ok(a, c) and ok(c, zs[0])]
+                ds = sorted([q for q in home if q != cs[0]],
+                            key=lambda q: 0 if topo.die(cores[q]) != topo.die(cores[cs[0]]) else 1)
+                bd = (zs[0], a, b, cs[0], ds[0])
+                as_z[bd[0]], as_a[a], as_b[b], as_c[bd[3]], as_d[bd[4]] = bd, bd, bd, bd, bd
 
     lo_m, all_m = None, 0
-    for d in cores:
-        if d != core:
-            m = topo.mask(core, d)
+    for q in cores:
+        if q != core:
+            m = topo.mask(core, q)
             lo_m = m if lo_m is None else (lo_m & m)
             all_m |= m
     hi_m = all_m & ~lo_m
@@ -72,21 +77,21 @@ def rank_program(g, core, T, topo):
             queue.wait_ge(T.sem[sem], val)
             waited[(qname, sem)] = val
 
-    def send(items):
-        far = [it for it in items if topo.chip(cores[it[1]]) != topo.chip(core)]
-        near = [it for it in items if topo.chip(cores[it[1]]) == topo.chip(core)]
-        assert len(far) <= 1 and 1 <= len(items) <= 2
+    def send(src, dests, sem):
+        far = [q for q in dests if far_from(q[0])]
+        near = [q for q in dests if not far_from(q[0])]
+        assert len(far) <= 1 and 1 <= len(dests) <= 2
         if far:
-            pairs = [(far[0], lo_m)] + [(it, hi_m) for it in near]
+            pairs = [(far[0], lo_m)] + [(q, hi_m) for q in near]
         elif len(near) == 2:
             pairs = [(near[0], lo_m), (near[1], hi_m)]
         else:
             pairs = [(near[0], hi_m)]
         trs = []
-        for (src, q, dst, sem), m in pairs:
+        for (q, ap), m in pairs:
             rid, pid, _se = topo.addr(cores[q])
             trs.append(RemoteDMATransfer(dst_ids=[DstId(rid=rid, pnc=pid)], dma_engine_mask=m,
-                                         remote_sem=T.sem[sem], src=src, dst=dst))
+                                         remote_sem=T.sem[sem], src=src, dst=ap))
             sent[0] += E
         g.remote_dma_fused(trs, local_sem=T.sem.sent)
 
@@ -97,29 +102,34 @@ def rank_program(g, core, T, topo):
     g.scalar.dma_start(T.wsb[:], T.w[:]).then_inc(T.sem.ldw, 16)
 
     need("g", g, "ldx", 16)
-    items = [(T.xin[:, col(own)], q, T.xin[:, col(ti(q, r))], "sx%d" % ti(q, r))
-             for q in users[r] if ok(r, q) and q not in as_b]
+    dests = [(q, T.xin[:, col(ti(q, r))]) for q in users[r] if ok(r, q) and q not in as_b]
     if r in as_a:
-        items.append((T.xin[:, col(own)], as_a[r][3], T.ax[:], "s_ax"))
-    send(items)
+        dests.append((as_a[r][3], T.ax[:]))
+    if r in as_b:
+        dests.append((as_b[r][4], T.dx[:]))
+    send(T.xin[:, col(own)], dests, "X%d" % r)
     if r in as_a:
-        z, a, b, c = as_a[r]
+        z, a, b, c, d = as_a[r]
         need("g", g, "ldw", 16)
-        send([(T.wsb[:, col(ti(a, b))], z, T.zw[:], "s_zw"), (T.wsb[:, col(ti(a, b))], c, T.aw[:], "s_aw")])
+        send(T.wsb[:, col(ti(a, b))], [(z, T.zw[:]), (b, T.zw[:])], "W%d" % r)
     if r in as_b:
         need("g", g, "ldw", 16)
-        send([(T.wsb[:], as_b[r][3], T.wb[:], "s_wb")])
+        send(T.wsb[:], [(as_b[r][3], T.wb[:])], "W%d" % r)
     if r in as_c:
-        z, a, b, c = as_c[r]
-        need("g", g, "sx%d" % ti(c, b), E)
-        send([(T.xin[:, col(ti(c, b))], z, T.bx[:], "s_bx")])
+        z, a, b, c, d = as_c[r]
+        need("g", g, "X%d" % b, E)
+        send(T.xin[:, col(ti(c, b))], [(z, T.bx[:])], "F%d" % r)
+    if r in as_d:
+        z, a, b, c, d = as_d[r]
+        need("g", g, "X%d" % b, E)
+        send(T.dx[:], [(a, T.bx[:])], "F%d" % r)
     if r not in as_b:
         need("g", g, "v_h", 1)
-        send([(T.hin[:, col(own)], q, T.hin[:, col(ti(q, r))], "sh%d" % ti(q, r)) for q in users[r]])
+        send(T.hin[:, col(own)], [(q, T.hin[:, col(ti(q, r))]) for q in users[r]], "H%d" % r)
     if r in as_c:
-        z, a, b, c = as_c[r]
+        z, a, b, c, d = as_c[r]
         need("g", g, "v_b", 1)
-        send([(T.hp[:], a, T.hp[:], "s_hp"), (T.hp[:], b, T.hp[:], "s_hp")])
+        send(T.hb[:], [(a, T.hb[:]), (b, T.hb[:])], "P%d" % r)
     g.wait_ge(T.sem.sent, sent[0])
 
     def group(out, terms, done):
@@ -128,11 +138,8 @@ def rank_program(g, core, T, topo):
             for s, v in ws:
                 need("t", te, s, v)
             ins = te.matmul(out, lhsT, rhs, k == 0, k == len(terms) - 1)
-            if done is not None and k == len(terms) - 1:
+            if k == len(terms) - 1:
                 ins.then_inc(T.sem[done], 1)
-
-    def far_from(j):
-        return topo.chip(cores[j]) != topo.chip(core)
 
     need("t", te, "ldw", 16)
     if r not in as_b:
@@ -141,29 +148,37 @@ def rank_program(g, core, T, topo):
             if j == r:
                 terms.append((0, T.wsb[:, col(i)], T.xin[:, col(i)], [("ldx", 16)]))
             elif ok(j, r):
-                terms.append((2 if far_from(j) else 1, T.wsb[:, col(i)], T.xin[:, col(i)], [("sx%d" % i, E)]))
+                terms.append((2 if far_from(j) else 1, T.wsb[:, col(i)], T.xin[:, col(i)], [("X%d" % j, E)]))
         group(T.ph[:, 0:K], terms, "m_h")
         ve.wait_ge(T.sem.m_h, 1)
         ve.tensor_copy(T.hin[:, col(own)], T.ph[:, 0:K]).then_inc(T.sem.v_h, 1)
     if r in as_c:
-        z, a, b, c = as_c[r]
-        xb = T.xin[:, col(ti(c, b))]
-        xb_w = ("sx%d" % ti(c, b), E)
+        z, a, b, c, d = as_c[r]
+        wb_w = ("W%d" % b, E)
         terms = []
         for i, j in enumerate(M[b]):
             if j == b:
-                terms.append((0, T.wb[:, col(i)], xb, [("s_wb", E), xb_w]))
+                terms.append((0, T.wb[:, col(i)], T.xin[:, col(ti(c, b))], [wb_w, ("X%d" % b, E)]))
             elif j == c:
-                terms.append((1, T.wb[:, col(i)], T.xin[:, col(own)], [("s_wb", E), ("ldx", 16)]))
+                terms.append((1, T.wb[:, col(i)], T.xin[:, col(own)], [wb_w, ("ldx", 16)]))
             else:
                 assert j == a
-                terms.append((2, T.wb[:, col(i)], T.ax[:], [("s_wb", E), ("s_ax", E)]))
-        group(T.pb[:, 0:K], terms, None)
-        group(T.pb[:, K:2 * K], [(0, T.aw[:], xb, [("s_aw", E), xb_w])], "m_b")
+                terms.append((2, T.wb[:, col(i)], T.ax[:], [wb_w, ("X%d" % a, E)]))
+        group(T.pb[:, 0:K], terms, "m_b")
         ve.wait_ge(T.sem.m_b, 1)
-        ve.tensor_copy(T.hp[:], T.pb[:, 0:2 * K]).then_inc(T.sem.v_b, 1)
+        ve.tensor_copy(T.hb[:], T.pb[:, 0:K]).then_inc(T.sem.v_b, 1)
+    pa = None
     if r in as_z:
-        group(T.pp[:, 0:K], [(0, T.zw[:], T.bx[:], [("s_zw", E), ("s_bx", E)])], "m_p")
+        z, a, b, c, d = as_z[r]
+        pa = (T.zw[:], T.bx[:], [("W%d" % a, E), ("F%d" % c, E)])
+    if r in as_a:
+        z, a, b, c, d = as_a[r]
+        pa = (T.wsb[:, col(ti(a, b))], T.bx[:], [("F%d" % d, E)])
+    if r in as_b:
+        z, a, b, c, d = as_b[r]
+        pa = (T.zw[:], T.xin[:, col(own)], [("ldx", 16), ("W%d" % a, E)])
+    if pa is not None:
+        group(T.pp[:, 0:K], [(0,) + pa], "m_p")
         ve.wait_ge(T.sem.m_p, 1)
         ve.tensor_copy(T.zp[:], T.pp[:, 0:K]).then_inc(T.sem.v_p, 1)
 
@@ -171,19 +186,17 @@ def rank_program(g, core, T, topo):
     for i, j in enumerate(M[r]):
         w_i = T.wsb[:, col(i)]
         if j in as_b:
-            if r == as_b[j][3]:
-                terms.append((1, w_i, T.hp[:, 0:K], [("v_b", 1)]))
+            c = as_b[j][3]
+            if r == c:
+                terms.append((1, w_i, T.hb[:], [("v_b", 1)]))
             else:
-                terms.append((5, w_i, T.hp[:, 0:K], [("s_hp", E)]))
+                terms.append((5, w_i, T.hb[:], [("P%d" % c, E)]))
         elif j == r:
             terms.append((0, w_i, T.hin[:, col(i)], [("v_h", 1)]))
         else:
-            terms.append((3 if far_from(j) else 2, w_i, T.hin[:, col(i)], [("sh%d" % i, E)]))
+            terms.append((3 if far_from(j) else 2, w_i, T.hin[:, col(i)], [("H%d" % j, E)]))
         if j in as_a:
-            if r == as_a[j][0]:
-                terms.append((4, w_i, T.zp[:], [("v_p", 1)]))
-            else:
-                terms.append((5, w_i, T.hp[:, K:2 * K], [("s_hp", E)]))
+            terms.append((4, w_i, T.zp[:], [("v_p", 1)]))
     group(T.py[:, 0:K], terms, "m_y")
     ve.wait_ge(T.sem.m_y, 1)
     ve.tensor_copy(T.yo[:], T.py[:, 0:K]).then_inc(T.sem.v_y, 1)

from concourse.bass import DstId, RemoteDMATransfer

K = 128
N = 9

SCRATCH = {
    "wsb": ("sbuf", [K, 3 * K], "bfloat16"),
    "xin": ("sbuf", [K, 3 * K], "bfloat16"),
    "hin": ("sbuf", [K, 3 * K], "bfloat16"),
    "hb": ("sbuf", [K, K], "bfloat16"),
    "ax": ("sbuf", [K, K], "bfloat16"),
    "wb": ("sbuf", [K, 3 * K], "bfloat16"),
    "zw": ("sbuf", [K, K], "bfloat16"),
    "bx": ("sbuf", [K, K], "bfloat16"),
    "dx": ("sbuf", [K, K], "bfloat16"),
    "zp": ("sbuf", [K, K], "bfloat16"),
    "yo": ("sbuf", [K, K], "bfloat16"),
    "ph": ("psum", [K, 512], "float32"),
    "pb": ("psum", [K, 512], "float32"),
    "pp": ("psum", [K, 512], "float32"),
    "py": ("psum", [K, 512], "float32"),
}
SEMAPHORES = (["ldx", "ldw", "st", "sent", "m_h", "m_b", "m_p", "m_y", "v_h", "v_b", "v_p", "v_y"]
              + ["%s%d" % (k, j) for k in "XWFHP" for j in range(N)])


def rank_program(g, core, T, topo):
    r = T.rank_of(core)
    if r is None:
        return
    M = T.tables["MASK"]
    cores = T.cores
    n = len(cores)

    def ok(s, d):
        return topo.may_write(cores[s], cores[d])

    def ti(q, j):
        return M[q].index(j)

    def col(i):
        return slice(i * K, (i + 1) * K)

    def far_from(j):
        return topo.chip(cores[j]) != topo.chip(core)

    users = [[q for q in range(n) if j in M[q] and q != j] for j in range(n)]

    as_a, as_b, as_c, as_z, as_d = {}, {}, {}, {}, {}
    for a in range(n):
        for b in M[a]:
            if b != a and not ok(b, a):
                zs = [q for q in users[a] if q != b]
                assert len(zs) == 1
                home = [q for q in range(n) if q != b and topo.chip(cores[q]) == topo.chip(cores[b]) and ok(q, a)]
                cs = [c for c in home if c in users[b] and ok(a, c) and ok(c, zs[0])]
                ds = sorted([q for q in home if q != cs[0]],
                            key=lambda q: 0 if topo.die(cores[q]) != topo.die(cores[cs[0]]) else 1)
                bd = (zs[0], a, b, cs[0], ds[0])
                as_z[bd[0]], as_a[a], as_b[b], as_c[bd[3]], as_d[bd[4]] = bd, bd, bd, bd, bd

    lo_m, all_m = None, 0
    for q in cores:
        if q != core:
            m = topo.mask(core, q)
            lo_m = m if lo_m is None else (lo_m & m)
            all_m |= m
    hi_m = all_m & ~lo_m
    E = bin(lo_m).count("1")
    assert bin(hi_m).count("1") == E

    sent = [0]
    waited = {}

    def need(qname, queue, sem, val):
        if waited.get((qname, sem), 0) < val:
            queue.wait_ge(T.sem[sem], val)
            waited[(qname, sem)] = val

    def send(src, dests, sem):
        far = [q for q in dests if far_from(q[0])]
        near = [q for q in dests if not far_from(q[0])]
        assert len(far) <= 1 and 1 <= len(dests) <= 2
        if far:
            pairs = [(far[0], lo_m)] + [(q, hi_m) for q in near]
        elif len(near) == 2:
            pairs = [(near[0], lo_m), (near[1], hi_m)]
        else:
            pairs = [(near[0], hi_m)]
        trs = []
        for (q, ap), m in pairs:
            rid, pid, _se = topo.addr(cores[q])
            trs.append(RemoteDMATransfer(dst_ids=[DstId(rid=rid, pnc=pid)], dma_engine_mask=m,
                                         remote_sem=T.sem[sem], src=src, dst=ap))
            sent[0] += E
        g.remote_dma_fused(trs, local_sem=T.sem.sent)

    own = ti(r, r)
    te, ve = g.tensor, g.vector

    g.sync.dma_start(T.xin[:, col(own)], T.x[:]).then_inc(T.sem.ldx, 16)
    g.scalar.dma_start(T.wsb[:], T.w[:]).then_inc(T.sem.ldw, 16)

    need("g", g, "ldx", 16)
    dests = [(q, T.xin[:, col(ti(q, r))]) for q in users[r] if ok(r, q) and q not in as_b]
    if r in as_a:
        dests.append((as_a[r][3], T.ax[:]))
    if r in as_b:
        dests.append((as_b[r][4], T.dx[:]))
    send(T.xin[:, col(own)], dests, "X%d" % r)
    if r in as_a:
        z, a, b, c, d = as_a[r]
        need("g", g, "ldw", 16)
        send(T.wsb[:, col(ti(a, b))], [(z, T.zw[:]), (b, T.zw[:])], "W%d" % r)
    if r in as_b:
        need("g", g, "ldw", 16)
        send(T.wsb[:], [(as_b[r][3], T.wb[:])], "W%d" % r)
    if r in as_c:
        z, a, b, c, d = as_c[r]
        need("g", g, "X%d" % b, E)
        send(T.xin[:, col(ti(c, b))], [(z, T.bx[:])], "F%d" % r)
    if r in as_d:
        z, a, b, c, d = as_d[r]
        need("g", g, "X%d" % b, E)
        send(T.dx[:], [(a, T.bx[:])], "F%d" % r)
    if r not in as_b:
        need("g", g, "v_h", 1)
        send(T.hin[:, col(own)], [(q, T.hin[:, col(ti(q, r))]) for q in users[r]], "H%d" % r)
    if r in as_c:
        z, a, b, c, d = as_c[r]
        need("g", g, "v_b", 1)
        send(T.hb[:], [(a, T.hb[:]), (b, T.hb[:])], "P%d" % r)
    g.wait_ge(T.sem.sent, sent[0])

    def group(out, terms, done):
        terms = sorted(terms, key=lambda t: t[0])
        for k, (_o, lhsT, rhs, ws) in enumerate(terms):
            for s, v in ws:
                need("t", te, s, v)
            ins = te.matmul(out, lhsT, rhs, k == 0, k == len(terms) - 1)
            if k == len(terms) - 1:
                ins.then_inc(T.sem[done], 1)

    need("t", te, "ldw", 16)
    if r not in as_b:
        terms = []
        for i, j in enumerate(M[r]):
            if j == r:
                terms.append((0, T.wsb[:, col(i)], T.xin[:, col(i)], [("ldx", 16)]))
            elif ok(j, r):
                terms.append((2 if far_from(j) else 1, T.wsb[:, col(i)], T.xin[:, col(i)], [("X%d" % j, E)]))
        group(T.ph[:, 0:K], terms, "m_h")
        ve.wait_ge(T.sem.m_h, 1)
        ve.tensor_copy(T.hin[:, col(own)], T.ph[:, 0:K]).then_inc(T.sem.v_h, 1)
    if r in as_c:
        z, a, b, c, d = as_c[r]
        wb_w = ("W%d" % b, E)
        terms = []
        for i, j in enumerate(M[b]):
            if j == b:
                terms.append((0, T.wb[:, col(i)], T.xin[:, col(ti(c, b))], [wb_w, ("X%d" % b, E)]))
            elif j == c:
                terms.append((1, T.wb[:, col(i)], T.xin[:, col(own)], [wb_w, ("ldx", 16)]))
            else:
                assert j == a
                terms.append((2, T.wb[:, col(i)], T.ax[:], [wb_w, ("X%d" % a, E)]))
        group(T.pb[:, 0:K], terms, "m_b")
        ve.wait_ge(T.sem.m_b, 1)
        ve.tensor_copy(T.hb[:], T.pb[:, 0:K]).then_inc(T.sem.v_b, 1)
    pa = None
    if r in as_z:
        z, a, b, c, d = as_z[r]
        pa = (T.zw[:], T.bx[:], [("W%d" % a, E), ("F%d" % c, E)])
    if r in as_a:
        z, a, b, c, d = as_a[r]
        pa = (T.wsb[:, col(ti(a, b))], T.bx[:], [("F%d" % d, E)])
    if r in as_b:
        z, a, b, c, d = as_b[r]
        pa = (T.zw[:], T.xin[:, col(own)], [("ldx", 16), ("W%d" % a, E)])
    if pa is not None:
        group(T.pp[:, 0:K], [(0,) + pa], "m_p")
        ve.wait_ge(T.sem.m_p, 1)
        ve.tensor_copy(T.zp[:], T.pp[:, 0:K]).then_inc(T.sem.v_p, 1)

    terms = []
    for i, j in enumerate(M[r]):
        w_i = T.wsb[:, col(i)]
        if j in as_b:
            c = as_b[j][3]
            if r == c:
                terms.append((1, w_i, T.hb[:], [("v_b", 1)]))
            else:
                terms.append((5, w_i, T.hb[:], [("P%d" % c, E)]))
        elif j == r:
            terms.append((0, w_i, T.hin[:, col(i)], [("v_h", 1)]))
        else:
            terms.append((3 if far_from(j) else 2, w_i, T.hin[:, col(i)], [("H%d" % j, E)]))
        if j in as_a:
            terms.append((4, w_i, T.zp[:], [("v_p", 1)]))
    group(T.py[:, 0:K], terms, "m_y")
    ve.wait_ge(T.sem.m_y, 1)
    ve.tensor_copy(T.yo[:], T.py[:, 0:K]).then_inc(T.sem.v_y, 1)

    g.sync.wait_ge(T.sem.v_y, 1)
    g.sync.dma_start(T.y[:], T.yo[:]).then_inc(T.sem.st, 16)
    g.sync.wait_ge(T.sem.st, 16)
